import numpy as np
import ml_dtypes


def mxq(x, axis, fmt="e4m3"):
    dtype, down = {"e4m3": (ml_dtypes.float8_e4m3fn, 7), "e5m2": (ml_dtypes.float8_e5m2, 14)}[fmt]
    v = np.moveaxis(np.asarray(x, np.float32).astype(ml_dtypes.bfloat16).astype(np.float64), axis, -1)
    blocks = v.reshape(v.shape[:-1] + (-1, 32))
    amax = np.abs(blocks).max(-1, keepdims=True)
    byte = np.maximum(np.where(amax > 0, np.frexp(amax)[1] - 1 + 127, 0) - down, 1)
    scale = np.exp2(byte - 127.0)
    codes = (blocks / scale).astype(np.float32).astype(dtype).astype(np.float64)
    return np.moveaxis((codes * scale).reshape(v.shape), -1, axis)


WIDE = False


def mx_kscale(k):
    if not WIDE:
        return np.ones(k)
    levels = np.array([10, -10, 5, -5, 0])
    if k % 512:
        return np.exp2(np.random.permutation(np.resize(levels, k // 32))).repeat(32)
    a = np.empty((k // 512, 16))
    for p in range(k // 512):
        a[p, :8] = np.random.permutation(np.resize(levels, 8))
        for g in range(8):
            far = levels[np.abs(levels - a[p, g]) >= 10]
            a[p, g + 8] = far[np.random.randint(len(far))]
    return np.exp2(a.ravel()).repeat(32)


def f64(x):
    return np.asarray(x).astype(np.float64)


def striped(idx):
    return np.tile(idx.reshape(-1, 16).T, (8, 1)).astype(np.uint16)


def unstriped(offs):
    return offs[:16].T.reshape(-1).astype(np.int64)


def pack_weight(w):
    k, n = w.shape
    w = f64(np.asarray(w, np.float32).astype(ml_dtypes.bfloat16)).reshape(k // 32, 32, n)
    amax = np.abs(w).max(1)
    byte = np.clip(np.where(amax > 0, np.frexp(amax)[1] - 1 + 127 - 7, 1), 1, 254)
    scaled = (w * np.exp2(127.0 - byte)[:, None, :]).reshape(k, n).astype(np.float32)
    words = np.ascontiguousarray(scaled.reshape(k // 512, 128, 4, n).transpose(0, 1, 3, 2)).astype(ml_dtypes.float8_e4m3fn).view(np.uint8)
    return words, np.ascontiguousarray(byte.astype(np.uint8).reshape(k // 512, 16, n))


def unpack_weight(words, scales):
    g, p, n, _ = words.shape
    vals = np.ascontiguousarray(words).view(ml_dtypes.float8_e4m3fn).astype(np.float64) * np.repeat(np.exp2(scales.astype(np.float64) - 127.0), 8, axis=1)[..., None]
    return vals.transpose(0, 1, 3, 2).reshape(g * 512, n)


K, T, S, N, H, W = 512, 2048, 512, 128, 512, 1024


def setup_inputs():
    n = np.random.standard_normal
    s = mx_kscale(K)[:, None]
    u = mx_kscale(H)
    packed_xT = pack_weight(n((K, T)) * s)
    packed_eT = pack_weight(n((K, W)) * s)
    return {
        "x_words": packed_xT[0],
        "x_scales": packed_xT[1],
        "w1": (n((K, H)) / np.sqrt(K) / s).astype(np.float32),
        "e_words": packed_eT[0],
        "e_scales": packed_eT[1],
        "w2": (n((K, H)) / np.sqrt(K) / s).astype(np.float32),
        "unit": (np.random.uniform(0.6, 1.4, (H, 1)) * u[:, None]).astype(np.float32),
        "w3": (n((H, N)) / np.sqrt(H) / u[:, None]).astype(np.float32),
        "offs": striped(np.random.permutation(T)[:S]),
        "old1": striped(np.random.permutation(W)[:S]),
        "org": striped(np.random.permutation(S)),
        "sib": striped(np.random.permutation(S)),
    }


def reference(x_words, x_scales, w1, e_words, e_scales, w2, unit, w3, offs, old1, org, sib):
    xq = unpack_weight(x_words, x_scales)[:, unstriped(offs)]
    y = mxq(f64(w1), 0, "e4m3").T @ xq
    e_old1 = unpack_weight(e_words, e_scales)[:, unstriped(old1)]
    ye = mxq(f64(w2), 0, "e4m3").T @ e_old1
    eo = ye[:, unstriped(org)]
    dif = y - eo
    ds = dif[:, unstriped(sib)]
    hid = f64(unit) * np.maximum(dif, -0.8 * ds)
    return mxq(f64(w3), 0, "e4m3").T @ mxq(hid, 0, "e4m3")

@@ -1,0 +1,156 @@
+from contextlib import ExitStack
+
+import concourse.mybir as mybir
+
+F32 = mybir.dt.float32
+BF16 = mybir.dt.bfloat16
+I32 = mybir.dt.int32
+U32 = mybir.dt.uint32
+U16 = mybir.dt.uint16
+U8 = mybir.dt.uint8
+FP8X4 = mybir.dt.float8_e4m3fn_x4
+ALU = mybir.AluOpType
+ACT = mybir.ActivationFunctionType
+
+P = 128
+PACK = 4
+K, T, S, N, H, W = 512, 2048, 512, 128, 512, 1024
+STRIPE = 16
+HALF = S // 2
+CHUNKS = ((0, 256), (256, 384), (384, 512))
+ON_VECTOR = ((2, 0), (2, 1), (3, 1))
+FLOPS = 2 * K * H * S * 2 + 2 * H * N * S
+
+
+def tile_picked_ycodrev_sib_p_kernel(tc, x_words, x_scales, w1, e_words, e_scales, w2, unit, w3, offs, old1, org, sib, out):
+    nc = tc.nc
+    with ExitStack() as ctx:
+        keep = ctx.enter_context(tc.tile_pool(name="keep", bufs=1))
+        psum = ctx.enter_context(tc.psum_pool(name="psum", bufs=1))
+
+        def sbuf(shape, dtype, name, tag=None):
+            return keep.tile(shape, dtype, name=name, tag=tag or name, align_bytes=64)
+
+        def load_list(src, name):
+            t = keep.tile([P, S // STRIPE], U16, name=name)
+            nc.sync.dma_start(t[:], src)
+            return t
+
+        def load_words(src, cols, name):
+            t = sbuf([P, cols], U32, name)
+            nc.sync.dma_start(t[:].bitcast(I32), src[0].rearrange("p n t -> p (n t)").bitcast(I32))
+            return t
+
+        def load_rows(src, cols, name):
+            t = sbuf([P, PACK, cols], F32, name)
+            nc.sync.dma_start(t[:], src.rearrange("(p j) c -> p j c", j=PACK))
+            return t
+
+        def gather(table, lst, dtype, name, tag=None):
+            t = sbuf([P, S], dtype, name, tag)
+            nc.vector.tensor_copy(t[:], table[:].indirect(lst[:]))
+            return t
+
+        def pair_views(raw, u, rounded):
+            src = raw[:].rearrange("p j (m t) -> p m j t", t=PACK)[:, :, :, 2 * u : 2 * u + 2]
+            return rounded.rearrange("p (t m j) -> p m j t", t=2, j=PACK), src
+
+        def quantize(src, cols, name, tag=None):
+            codes = sbuf([P, cols], U32, name + "_codes", tag)
+            scales = sbuf([P, cols], U8, name + "_scales")
+            nc.vector.quantize_mx(out=codes[:].bitcast(FP8X4), scales=scales[:], in_=src)
+            return codes, scales
+
+        def product(bank, wq, cols, words, scales):
+            nc.tensor.matmul_mx(out=bank, lhsT=wq[0][:, cols].bitcast(FP8X4), lhsT_scale=wq[1][:, cols],
+                                rhs=words[:].bitcast(FP8X4), rhs_scale=scales[:], start=True, stop=True)
+
+        xs_tab = sbuf([P, T], U8, "xs_tab", "chain")
+        unit_t = keep.tile([P, PACK], F32, name="unit_t")
+        nc.gpsimd.dma_start(unit_t[:], unit.rearrange("(p t) o -> p (t o)", t=PACK))
+        nc.gpsimd.memset(xs_tab[:].bitcast(I32), 0)
+        es_tab = sbuf([P, W], U8, "es_tab")
+        for q in range(4):
+            rows = e_scales[0, 4 * q : 4 * q + 4, :].bitcast(I32)
+            nc.sync.dma_start(es_tab[32 * q : 32 * q + 32, :].bitcast(I32), rows.unsqueeze(0).to_broadcast([8, 4, W // 4]))
+        old1_t = load_list(old1, "old1_t")
+        ew_tab = load_words(e_words, W, "ew_tab")
+        w2_raw = load_rows(w2, H, "w2_raw")
+        offs_t = load_list(offs, "offs_t")
+        for q in range(4):
+            nc.scalar.dma_start(xs_tab[32 * q : 32 * q + 4, :].bitcast(I32), x_scales[0, 4 * q : 4 * q + 4, :].bitcast(I32))
+        w1_raw = load_rows(w1, H, "w1_raw")
+        org_t = load_list(org, "org_t")
+        sib_t = load_list(sib, "sib_t")
+        xw_tab = load_words(x_words, T, "xw_tab")
+        w3_raw = load_rows(w3, N, "w3_raw")
+
+        unit_abs = keep.tile([P, PACK], F32, name="unit_abs")
+        nc.scalar.activation(unit_abs[:], unit_t[:], ACT.Abs)
+        unit_ge = keep.tile([P, PACK], F32, name="unit_ge")
+        nc.gpsimd.tensor_scalar(unit_ge[:], unit_t[:], 0.0, None, ALU.is_ge)
+        unit_sign = keep.tile([P, PACK], F32, name="unit_sign")
+        nc.gpsimd.tensor_scalar(unit_sign[:], unit_ge[:], 2.0, -1.0, ALU.mult, ALU.add)
+
+        es = gather(es_tab, old1_t, U8, "es")
+        ew = gather(ew_tab, old1_t, U32, "ew")
+        w2_b0 = sbuf([P, 2 * P * PACK], BF16, "w2_b0")
+        w2_b1 = sbuf([P, 2 * P * PACK], BF16, "w2_b1")
+        nc.vector.tensor_copy(*pair_views(w2_raw, 0, w2_b0[:]))
+        nc.scalar.copy(*pair_views(w2_raw, 1, w2_b1[:]))
+        w2_q = (quantize(w2_b0[:], 2 * P, "w2_q0"), quantize(w2_b1[:], 2 * P, "w2_q1"))
+
+        ye_sb = []
+        for t in range(PACK):
+            bank = psum.tile([P, S], F32, name=f"ye{t}", tag=f"bank{t}")
+            product(bank[:], w2_q[t // 2], slice((t % 2) * P, (t % 2 + 1) * P), ew, es)
+            sb = sbuf([P, S], F32, f"ye_sb{t}")
+            nc.scalar.activation(sb[:], bank[:], ACT.Copy, scale=unit_abs[:, t : t + 1])
+            ye_sb.append(sb)
+
+        xs = gather(xs_tab, offs_t, U8, "xs", "w2_b1")
+        w1_b = sbuf([P, PACK * P * PACK], BF16, "w1_b", "chain")
+        pairs = [w1_b[:, u * 2 * P * PACK : (u + 1) * 2 * P * PACK] for u in range(2)]
+        for u in range(2):
+            nc.vector.tensor_copy(*pair_views(w1_raw, u, pairs[u]))
+        w1_q = [quantize(pairs[u], 2 * P, f"w1_q{u}") for u in range(2)]
+        xw = gather(xw_tab, offs_t, U32, "xw", "chain")
+
+        w3_b = sbuf([P, N, PACK], BF16, "w3_b")
+        nc.gpsimd.tensor_tensor(w3_b[:], w3_raw[:].rearrange("p j m -> p m j"),
+                                unit_sign[:].unsqueeze(1).to_broadcast([P, N, PACK]), ALU.mult)
+
+        eo = [sbuf([P, S], F32, f"eo{t}") for t in range(PACK)]
+        dif = sbuf([P, PACK * S], F32, "dif")
+        for t in range(PACK):
+            for h in range(2):
+                window = ye_sb[t][:].indirect(org_t[:, h * HALF // STRIPE : (h + 1) * HALF // STRIPE])
+                dst = eo[t][:, h * HALF : (h + 1) * HALF]
+                if (t, h) in ON_VECTOR:
+                    nc.vector.tensor_copy(dst, window)
+                else:
+                    nc.scalar.activation(dst, window, ACT.Copy)
+            bank = psum.tile([P, S], F32, name=f"y{t}", tag=f"bank{PACK + t}")
+            product(bank[:], w1_q[t // 2], slice((t % 2) * P, (t % 2 + 1) * P), xw, xs)
+            nc.vector.scalar_tensor_tensor(dif[:, t * S : (t + 1) * S], bank[:], unit_abs[:, t : t + 1], eo[t][:], ALU.mult, ALU.subtract)
+
+        w3_q = quantize(w3_b[:].rearrange("p m j -> p (m j)"), N, "w3_q", "eo3")
+
+        ds = []
+        for c, (lo, hi) in enumerate(CHUNKS):
+            width = hi - lo
+            ds.append(sbuf([P, PACK * width], F32, f"ds{c}"))
+            for t in range(PACK):
+                nc.scalar.activation(ds[c][:, t * width : (t + 1) * width], dif[:, t * S : (t + 1) * S].indirect(sib_t[:, lo // STRIPE : hi // STRIPE]), ACT.Copy, scale=-0.8)
+        for c, (lo, hi) in enumerate(CHUNKS):
+            width = hi - lo
+            hid = sbuf([P, width, PACK], BF16, f"hid{c}")
+            nc.vector.tensor_tensor(hid[:].rearrange("p (c i) t -> p c t i", i=2),
+                                    dif[:].rearrange("p (t c i) -> p c t i", t=PACK, i=2)[:, lo // 2 : hi // 2],
+                                    ds[c][:].rearrange("p (t c i) -> p c t i", t=PACK, i=2), ALU.max)
+            hid_q = quantize(hid[:].rearrange("p c t -> p (c t)"), width, f"hid_q{c}")
+            bank = psum.tile([P, width], F32, name=f"o{c}", tag=f"bank{c}")
+            product(bank[:], w3_q, slice(0, N), hid_q[0], hid_q[1])
+            res = sbuf([P, width], F32, f"res{c}")
+            nc.scalar.copy(res[:], bank[:])
+            nc.sync.dma_start(out[:, lo:hi], res[:])

@@ -18,7 +18,8 @@ K, T, S, N, H, W = 512, 2048, 512, 128, 512, 1024
 STRIPE = 16
 HALF = S // 2
 CHUNKS = ((0, 256), (256, 384), (384, 512))
-ON_VECTOR = ((2, 0), (2, 1), (3, 1))
+ORG_PLAN = (((True, 0, 256), (True, 256, 512)), ((False, 0, 512),), ((False, 0, 512),), ((False, 0, 512),))
+SIB_PLAN = ((False, 0, 0, 256), (False, 1, 0, 256), (False, 2, 0, 256), (False, 3, 0, 256), (True, 0, 256, 512), (False, 1, 256, 512), (False, 2, 256, 512), (False, 3, 256, 384), (False, 3, 384, 512))
 FLOPS = 2 * K * H * S * 2 + 2 * H * N * S
 
 
@@ -65,20 +66,20 @@ def tile_picked_ycodrev_sib_p_kernel(tc, x_words, x_scales, w1, e_words, e_scale
             nc.tensor.matmul_mx(out=bank, lhsT=wq[0][:, cols].bitcast(FP8X4), lhsT_scale=wq[1][:, cols],
                                 rhs=words[:].bitcast(FP8X4), rhs_scale=scales[:], start=True, stop=True)
 
-        xs_tab = sbuf([P, T], U8, "xs_tab", "chain")
+        xs_tab = sbuf([P, T], U8, "xs_tab")
         unit_t = keep.tile([P, PACK], F32, name="unit_t")
         nc.gpsimd.dma_start(unit_t[:], unit.rearrange("(p t) o -> p (t o)", t=PACK))
         nc.gpsimd.memset(xs_tab[:].bitcast(I32), 0)
+        ew_tab = load_words(e_words, W, "ew_tab")
+        old1_t = load_list(old1, "old1_t")
         es_tab = sbuf([P, W], U8, "es_tab")
         for q in range(4):
             rows = e_scales[0, 4 * q : 4 * q + 4, :].bitcast(I32)
             nc.sync.dma_start(es_tab[32 * q : 32 * q + 32, :].bitcast(I32), rows.unsqueeze(0).to_broadcast([8, 4, W // 4]))
-        old1_t = load_list(old1, "old1_t")
-        ew_tab = load_words(e_words, W, "ew_tab")
         w2_raw = load_rows(w2, H, "w2_raw")
         offs_t = load_list(offs, "offs_t")
         for q in range(4):
-            nc.scalar.dma_start(xs_tab[32 * q : 32 * q + 4, :].bitcast(I32), x_scales[0, 4 * q : 4 * q + 4, :].bitcast(I32))
+            nc.sync.dma_start(xs_tab[32 * q : 32 * q + 4, :].bitcast(I32), x_scales[0, 4 * q : 4 * q + 4, :].bitcast(I32))
         w1_raw = load_rows(w1, H, "w1_raw")
         org_t = load_list(org, "org_t")
         sib_t = load_list(sib, "sib_t")
@@ -92,8 +93,8 @@ def tile_picked_ycodrev_sib_p_kernel(tc, x_words, x_scales, w1, e_words, e_scale
         unit_sign = keep.tile([P, PACK], F32, name="unit_sign")
         nc.gpsimd.tensor_scalar(unit_sign[:], unit_ge[:], 2.0, -1.0, ALU.mult, ALU.add)
 
-        es = gather(es_tab, old1_t, U8, "es")
         ew = gather(ew_tab, old1_t, U32, "ew")
+        es = gather(es_tab, old1_t, U8, "es")
         w2_b0 = sbuf([P, 2 * P * PACK], BF16, "w2_b0")
         w2_b1 = sbuf([P, 2 * P * PACK], BF16, "w2_b1")
         nc.vector.tensor_copy(*pair_views(w2_raw, 0, w2_b0[:]))
@@ -104,50 +105,55 @@ def tile_picked_ycodrev_sib_p_kernel(tc, x_words, x_scales, w1, e_words, e_scale
         for t in range(PACK):
             bank = psum.tile([P, S], F32, name=f"ye{t}", tag=f"bank{t}")
             product(bank[:], w2_q[t // 2], slice((t % 2) * P, (t % 2 + 1) * P), ew, es)
-            sb = sbuf([P, S], F32, f"ye_sb{t}")
-            nc.scalar.activation(sb[:], bank[:], ACT.Copy, scale=unit_abs[:, t : t + 1])
+            sb = sbuf([P, S + STRIPE], F32, f"ye_sb{t}")
+            nc.gpsimd.memset(sb[:, S:], 0.0)
+            nc.scalar.activation(sb[:, :S], bank[:], ACT.Copy, scale=unit_abs[:, t : t + 1])
             ye_sb.append(sb)
 
-        xs = gather(xs_tab, offs_t, U8, "xs", "w2_b1")
-        w1_b = sbuf([P, PACK * P * PACK], BF16, "w1_b", "chain")
-        pairs = [w1_b[:, u * 2 * P * PACK : (u + 1) * 2 * P * PACK] for u in range(2)]
+        xs = gather(xs_tab, offs_t, U8, "xs", "w2_raw")
+        w1_b = [sbuf([P, 2 * P * PACK], BF16, f"w1_b{u}", f"w2_b{u}") for u in range(2)]
         for u in range(2):
-            nc.vector.tensor_copy(*pair_views(w1_raw, u, pairs[u]))
-        w1_q = [quantize(pairs[u], 2 * P, f"w1_q{u}") for u in range(2)]
-        xw = gather(xw_tab, offs_t, U32, "xw", "chain")
-
-        w3_b = sbuf([P, N, PACK], BF16, "w3_b")
-        nc.gpsimd.tensor_tensor(w3_b[:], w3_raw[:].rearrange("p j m -> p m j"),
-                                unit_sign[:].unsqueeze(1).to_broadcast([P, N, PACK]), ALU.mult)
+            nc.vector.tensor_copy(*pair_views(w1_raw, u, w1_b[u][:]))
+        w1_q = [quantize(w1_b[u][:], 2 * P, f"w1_q{u}") for u in range(2)]
+        xw = gather(xw_tab, offs_t, U32, "xw", "w2_b0")
 
         eo = [sbuf([P, S], F32, f"eo{t}") for t in range(PACK)]
         dif = sbuf([P, PACK * S], F32, "dif")
         for t in range(PACK):
-            for h in range(2):
-                window = ye_sb[t][:].indirect(org_t[:, h * HALF // STRIPE : (h + 1) * HALF // STRIPE])
-                dst = eo[t][:, h * HALF : (h + 1) * HALF]
-                if (t, h) in ON_VECTOR:
-                    nc.vector.tensor_copy(dst, window)
+            for on_vector, lo, hi in ORG_PLAN[t]:
+                window = ye_sb[t][:].indirect(org_t[:, lo // STRIPE : hi // STRIPE])
+                if on_vector:
+                    nc.vector.tensor_copy(eo[t][:, lo:hi], window)
                 else:
-                    nc.scalar.activation(dst, window, ACT.Copy)
+                    nc.scalar.activation(eo[t][:, lo:hi], window, ACT.Copy)
             bank = psum.tile([P, S], F32, name=f"y{t}", tag=f"bank{PACK + t}")
             product(bank[:], w1_q[t // 2], slice((t % 2) * P, (t % 2 + 1) * P), xw, xs)
             nc.vector.scalar_tensor_tensor(dif[:, t * S : (t + 1) * S], bank[:], unit_abs[:, t : t + 1], eo[t][:], ALU.mult, ALU.subtract)
 
+        w3_b = sbuf([P, N, PACK], BF16, "w3_b", "eo0")
+        nc.gpsimd.tensor_tensor(w3_b[:], w3_raw[:].rearrange("p j m -> p m j"),
+                                unit_sign[:].unsqueeze(1).to_broadcast([P, N, PACK]), ALU.mult)
+
+        scaled = sbuf([P, S], F32, "scaled", "eo2")
+        nc.gpsimd.tensor_scalar(scaled[:], dif[:, 0:S], -0.8, 0.0, ALU.mult, ALU.add)
         w3_q = quantize(w3_b[:].rearrange("p m j -> p (m j)"), N, "w3_q", "eo3")
 
-        ds = []
-        for c, (lo, hi) in enumerate(CHUNKS):
-            width = hi - lo
-            ds.append(sbuf([P, PACK * width], F32, f"ds{c}"))
-            for t in range(PACK):
-                nc.scalar.activation(ds[c][:, t * width : (t + 1) * width], dif[:, t * S : (t + 1) * S].indirect(sib_t[:, lo // STRIPE : hi // STRIPE]), ACT.Copy, scale=-0.8)
+        ds = [sbuf([P, PACK * HALF], F32, f"ds{h}") for h in range(2)]
+        for on_vector, t, lo, hi in SIB_PLAN:
+            places = sib_t[:, lo // STRIPE : hi // STRIPE]
+            at = t * HALF + lo % HALF
+            dst = ds[lo // HALF][:, at : at + hi - lo]
+            if on_vector:
+                nc.vector.tensor_copy(dst, scaled[:].indirect(places))
+            else:
+                nc.scalar.activation(dst, dif[:, t * S : (t + 1) * S].indirect(places), ACT.Copy, scale=-0.8)
         for c, (lo, hi) in enumerate(CHUNKS):
             width = hi - lo
             hid = sbuf([P, width, PACK], BF16, f"hid{c}")
+            at = lo % HALF // 2
             nc.vector.tensor_tensor(hid[:].rearrange("p (c i) t -> p c t i", i=2),
                                     dif[:].rearrange("p (t c i) -> p c t i", t=PACK, i=2)[:, lo // 2 : hi // 2],
-                                    ds[c][:].rearrange("p (t c i) -> p c t i", t=PACK, i=2), ALU.max)
+                                    ds[lo // HALF][:].rearrange("p (t c i) -> p c t i", t=PACK, i=2)[:, at : at + width // 2], ALU.max)
             hid_q = quantize(hid[:].rearrange("p c t -> p (c t)"), width, f"hid_q{c}")
             bank = psum.tile([P, width], F32, name=f"o{c}", tag=f"bank{c}")
             product(bank[:], w3_q, slice(0, N), hid_q[0], hid_q[1])

@@ -18,7 +18,7 @@ K, T, S, N, H, W = 512, 2048, 512, 128, 512, 1024
 STRIPE = 16
 HALF = S // 2
 CHUNKS = ((0, 256), (256, 384), (384, 512))
-ORG_PLAN = (((True, 0, 256), (True, 256, 512)), ((False, 0, 512),), ((False, 0, 512),), ((False, 0, 512),))
+ORG_PLAN = (((True, 0, 256), (False, 256, 512)), ((False, 0, 512),), ((False, 0, 512),), ((False, 0, 512),))
 SIB_PLAN = ((False, 0, 0, 256), (False, 1, 0, 256), (False, 2, 0, 256), (False, 3, 0, 256), (True, 0, 256, 512), (False, 1, 256, 512), (False, 2, 256, 512), (False, 3, 256, 384), (False, 3, 384, 512))
 FLOPS = 2 * K * H * S * 2 + 2 * H * N * S
 
@@ -64,7 +64,7 @@ def tile_picked_ycodrev_sib_p_kernel(tc, x_words, x_scales, w1, e_words, e_scale
 
         def product(bank, wq, cols, words, scales):
             nc.tensor.matmul_mx(out=bank, lhsT=wq[0][:, cols].bitcast(FP8X4), lhsT_scale=wq[1][:, cols],
-                                rhs=words[:].bitcast(FP8X4), rhs_scale=scales[:], start=True, stop=True)
+                                rhs=words.bitcast(FP8X4), rhs_scale=scales, start=True, stop=True)
 
         xs_tab = sbuf([P, T], U8, "xs_tab")
         unit_t = keep.tile([P, PACK], F32, name="unit_t")
@@ -104,7 +104,7 @@ def tile_picked_ycodrev_sib_p_kernel(tc, x_words, x_scales, w1, e_words, e_scale
         ye_sb = []
         for t in range(PACK):
             bank = psum.tile([P, S], F32, name=f"ye{t}", tag=f"bank{t}")
-            product(bank[:], w2_q[t // 2], slice((t % 2) * P, (t % 2 + 1) * P), ew, es)
+            product(bank[:], w2_q[t // 2], slice((t % 2) * P, (t % 2 + 1) * P), ew[:], es[:])
             sb = sbuf([P, S + STRIPE], F32, f"ye_sb{t}")
             nc.gpsimd.memset(sb[:, S:], 0.0)
             nc.scalar.activation(sb[:, :S], bank[:], ACT.Copy, scale=unit_abs[:, t : t + 1])
@@ -115,7 +115,16 @@ def tile_picked_ycodrev_sib_p_kernel(tc, x_words, x_scales, w1, e_words, e_scale
         for u in range(2):
             nc.vector.tensor_copy(*pair_views(w1_raw, u, w1_b[u][:]))
         w1_q = [quantize(w1_b[u][:], 2 * P, f"w1_q{u}") for u in range(2)]
-        xw = gather(xw_tab, offs_t, U32, "xw", "w2_b0")
+        xw = sbuf([P, S], U32, "xw", "w2_b0")
+        halves = [slice(0, HALF), slice(HALF, S)]
+        for h in range(2):
+            nc.vector.tensor_copy(xw[:, halves[h]], xw_tab[:].indirect(offs_t[:, h * HALF // STRIPE : (h + 1) * HALF // STRIPE]))
+        y = [psum.tile([P, S], F32, name=f"y{t}", tag=f"bank{PACK + t}") for t in range(PACK)]
+        for h in range(2):
+            for t in range(2):
+                product(y[t][:, halves[h]], w1_q[0], slice(t * P, (t + 1) * P), xw[:, halves[h]], xs[:, halves[h]])
+        for t in range(2):
+            product(y[2 + t][:], w1_q[1], slice(t * P, (t + 1) * P), xw[:], xs[:])
 
         eo = [sbuf([P, S], F32, f"eo{t}") for t in range(PACK)]
         dif = sbuf([P, PACK * S], F32, "dif")
@@ -126,9 +135,7 @@ def tile_picked_ycodrev_sib_p_kernel(tc, x_words, x_scales, w1, e_words, e_scale
                     nc.vector.tensor_copy(eo[t][:, lo:hi], window)
                 else:
                     nc.scalar.activation(eo[t][:, lo:hi], window, ACT.Copy)
-            bank = psum.tile([P, S], F32, name=f"y{t}", tag=f"bank{PACK + t}")
-            product(bank[:], w1_q[t // 2], slice((t % 2) * P, (t % 2 + 1) * P), xw, xs)
-            nc.vector.scalar_tensor_tensor(dif[:, t * S : (t + 1) * S], bank[:], unit_abs[:, t : t + 1], eo[t][:], ALU.mult, ALU.subtract)
+            nc.vector.scalar_tensor_tensor(dif[:, t * S : (t + 1) * S], y[t][:], unit_abs[:, t : t + 1], eo[t][:], ALU.mult, ALU.subtract)
 
         w3_b = sbuf([P, N, PACK], BF16, "w3_b", "eo0")
         nc.gpsimd.tensor_tensor(w3_b[:], w3_raw[:].rearrange("p j m -> p m j"),
@@ -136,7 +143,6 @@ def tile_picked_ycodrev_sib_p_kernel(tc, x_words, x_scales, w1, e_words, e_scale
 
         scaled = sbuf([P, S], F32, "scaled", "eo2")
         nc.gpsimd.tensor_scalar(scaled[:], dif[:, 0:S], -0.8, 0.0, ALU.mult, ALU.add)
-        w3_q = quantize(w3_b[:].rearrange("p m j -> p (m j)"), N, "w3_q", "eo3")
 
         ds = [sbuf([P, PACK * HALF], F32, f"ds{h}") for h in range(2)]
         for on_vector, t, lo, hi in SIB_PLAN:
@@ -147,16 +153,27 @@ def tile_picked_ycodrev_sib_p_kernel(tc, x_words, x_scales, w1, e_words, e_scale
                 nc.vector.tensor_copy(dst, scaled[:].indirect(places))
             else:
                 nc.scalar.activation(dst, dif[:, t * S : (t + 1) * S].indirect(places), ACT.Copy, scale=-0.8)
-        for c, (lo, hi) in enumerate(CHUNKS):
-            width = hi - lo
-            hid = sbuf([P, width, PACK], BF16, f"hid{c}")
+        def larger(c):
+            lo, hi = CHUNKS[c]
+            hid = sbuf([P, hi - lo, PACK], BF16, f"hid{c}")
             at = lo % HALF // 2
             nc.vector.tensor_tensor(hid[:].rearrange("p (c i) t -> p c t i", i=2),
                                     dif[:].rearrange("p (t c i) -> p c t i", t=PACK, i=2)[:, lo // 2 : hi // 2],
-                                    ds[lo // HALF][:].rearrange("p (t c i) -> p c t i", t=PACK, i=2)[:, at : at + width // 2], ALU.max)
-            hid_q = quantize(hid[:].rearrange("p c t -> p (c t)"), width, f"hid_q{c}")
-            bank = psum.tile([P, width], F32, name=f"o{c}", tag=f"bank{c}")
-            product(bank[:], w3_q, slice(0, N), hid_q[0], hid_q[1])
-            res = sbuf([P, width], F32, f"res{c}")
+                                    ds[lo // HALF][:].rearrange("p (t c i) -> p c t i", t=PACK, i=2)[:, at : at + (hi - lo) // 2], ALU.max)
+            return hid
+
+        def finish(c, hid, w3_q):
+            lo, hi = CHUNKS[c]
+            hid_q = quantize(hid[:].rearrange("p c t -> p (c t)"), hi - lo, f"hid_q{c}")
+            bank = psum.tile([P, hi - lo], F32, name=f"o{c}", tag=f"bank{c}")
+            product(bank[:], w3_q, slice(0, N), hid_q[0][:], hid_q[1][:])
+            res = sbuf([P, hi - lo], F32, f"res{c}")
             nc.scalar.copy(res[:], bank[:])
             nc.sync.dma_start(out[:, lo:hi], res[:])
+
+        hid0 = larger(0)
+        w3_q = quantize(w3_b[:].rearrange("p m j -> p (m j)"), N, "w3_q", "ds0")
+        finish(0, hid0, w3_q)
+        rest = [larger(c) for c in (1, 2)]
+        for c in (1, 2):
+            finish(c, rest[c - 1], w3_q)

from contextlib import ExitStack

import concourse.mybir as mybir

F32 = mybir.dt.float32
BF16 = mybir.dt.bfloat16
I32 = mybir.dt.int32
U32 = mybir.dt.uint32
U16 = mybir.dt.uint16
U8 = mybir.dt.uint8
FP8X4 = mybir.dt.float8_e4m3fn_x4
ALU = mybir.AluOpType
ACT = mybir.ActivationFunctionType

P = 128
PACK = 4
K, T, S, N, H, W = 512, 2048, 512, 128, 512, 1024
STRIPE = 16
HALF = S // 2
CHUNKS = ((0, 256), (256, 384), (384, 512))
ORG_PLAN = (((True, 0, 256), (False, 256, 512)), ((False, 0, 512),), ((False, 0, 512),), ((False, 0, 512),))
SIB_PLAN = ((False, 0, 0, 256), (False, 1, 0, 256), (False, 2, 0, 256), (False, 3, 0, 256), (True, 0, 256, 512), (False, 1, 256, 512), (False, 2, 256, 512), (False, 3, 256, 384), (False, 3, 384, 512))
FLOPS = 2 * K * H * S * 2 + 2 * H * N * S


def tile_picked_ycodrev_sib_p_kernel(tc, x_words, x_scales, w1, e_words, e_scales, w2, unit, w3, offs, old1, org, sib, out):
    nc = tc.nc
    with ExitStack() as ctx:
        keep = ctx.enter_context(tc.tile_pool(name="keep", bufs=1))
        psum = ctx.enter_context(tc.psum_pool(name="psum", bufs=1))

        def sbuf(shape, dtype, name, tag=None):
            return keep.tile(shape, dtype, name=name, tag=tag or name, align_bytes=64)

        def load_list(src, name):
            t = keep.tile([P, S // STRIPE], U16, name=name)
            nc.sync.dma_start(t[:], src)
            return t

        def load_words(src, cols, name):
            t = sbuf([P, cols], U32, name)
            nc.sync.dma_start(t[:].bitcast(I32), src[0].rearrange("p n t -> p (n t)").bitcast(I32))
            return t

        def load_rows(src, cols, name):
            t = sbuf([P, PACK, cols], F32, name)
            nc.sync.dma_start(t[:], src.rearrange("(p j) c -> p j c", j=PACK))
            return t

        def gather(table, lst, dtype, name, tag=None):
            t = sbuf([P, S], dtype, name, tag)
            nc.vector.tensor_copy(t[:], table[:].indirect(lst[:]))
            return t

        def pair_views(raw, u, rounded):
            src = raw[:].rearrange("p j (m t) -> p m j t", t=PACK)[:, :, :, 2 * u : 2 * u + 2]
            return rounded.rearrange("p (t m j) -> p m j t", t=2, j=PACK), src

        def quantize(src, cols, name, tag=None):
            codes = sbuf([P, cols], U32, name + "_codes", tag)
            scales = sbuf([P, cols], U8, name + "_scales")
            nc.vector.quantize_mx(out=codes[:].bitcast(FP8X4), scales=scales[:], in_=src)
            return codes, scales

        def product(bank, wq, cols, words, scales):
            nc.tensor.matmul_mx(out=bank, lhsT=wq[0][:, cols].bitcast(FP8X4), lhsT_scale=wq[1][:, cols],
                                rhs=words.bitcast(FP8X4), rhs_scale=scales, start=True, stop=True)

        xs_tab = sbuf([P, T], U8, "xs_tab")
        unit_t = keep.tile([P, PACK], F32, name="unit_t")
        nc.gpsimd.dma_start(unit_t[:], unit.rearrange("(p t) o -> p (t o)", t=PACK))
        nc.gpsimd.memset(xs_tab[:].bitcast(I32), 0)
        ew_tab = load_words(e_words, W, "ew_tab")
        old1_t = load_list(old1, "old1_t")
        es_tab = sbuf([P, W], U8, "es_tab")
        for q in range(4):
            rows = e_scales[0, 4 * q : 4 * q + 4, :].bitcast(I32)
            nc.sync.dma_start(es_tab[32 * q : 32 * q + 32, :].bitcast(I32), rows.unsqueeze(0).to_broadcast([8, 4, W // 4]))
        w2_raw = load_rows(w2, H, "w2_raw")
        offs_t = load_list(offs, "offs_t")
        for q in range(4):
            nc.sync.dma_start(xs_tab[32 * q : 32 * q + 4, :].bitcast(I32), x_scales[0, 4 * q : 4 * q + 4, :].bitcast(I32))
        w1_raw = load_rows(w1, H, "w1_raw")
        org_t = load_list(org, "org_t")
        sib_t = load_list(sib, "sib_t")
        xw_tab = load_words(x_words, T, "xw_tab")
        w3_raw = load_rows(w3, N, "w3_raw")

        unit_abs = keep.tile([P, PACK], F32, name="unit_abs")
        nc.scalar.activation(unit_abs[:], unit_t[:], ACT.Abs)
        unit_ge = keep.tile([P, PACK], F32, name="unit_ge")
        nc.gpsimd.tensor_scalar(unit_ge[:], unit_t[:], 0.0, None, ALU.is_ge)
        unit_sign = keep.tile([P, PACK], F32, name="unit_sign")
        nc.gpsimd.tensor_scalar(unit_sign[:], unit_ge[:], 2.0, -1.0, ALU.mult, ALU.add)

        ew = gather(ew_tab, old1_t, U32, "ew")
        es = gather(es_tab, old1_t, U8, "es")
        w2_b0 = sbuf([P, 2 * P * PACK], BF16, "w2_b0")
        w2_b1 = sbuf([P, 2 * P * PACK], BF16, "w2_b1")
        nc.vector.tensor_copy(*pair_views(w2_raw, 0, w2_b0[:]))
        nc.scalar.copy(*pair_views(w2_raw, 1, w2_b1[:]))
        w2_q = (quantize(w2_b0[:], 2 * P, "w2_q0"), quantize(w2_b1[:], 2 * P, "w2_q1"))

        ye_sb = []
        for t in range(PACK):
            bank = psum.tile([P, S], F32, name=f"ye{t}", tag=f"bank{t}")
            product(bank[:], w2_q[t // 2], slice((t % 2) * P, (t % 2 + 1) * P), ew[:], es[:])
            sb = sbuf([P, S + STRIPE], F32, f"ye_sb{t}")
            nc.gpsimd.memset(sb[:, S:], 0.0)
            nc.scalar.activation(sb[:, :S], bank[:], ACT.Copy, scale=unit_abs[:, t : t + 1])
            ye_sb.append(sb)

        xs = gather(xs_tab, offs_t, U8, "xs", "w2_raw")
        w1_b = [sbuf([P, 2 * P * PACK], BF16, f"w1_b{u}", f"w2_b{u}") for u in range(2)]
        for u in range(2):
            nc.vector.tensor_copy(*pair_views(w1_raw, u, w1_b[u][:]))
        w1_q = [quantize(w1_b[u][:], 2 * P, f"w1_q{u}") for u in range(2)]
        xw = sbuf([P, S], U32, "xw", "w2_b0")
        halves = [slice(0, HALF), slice(HALF, S)]
        for h in range(2):
            nc.vector.tensor_copy(xw[:, halves[h]], xw_tab[:].indirect(offs_t[:, h * HALF // STRIPE : (h + 1) * HALF // STRIPE]))
        y = [psum.tile([P, S], F32, name=f"y{t}", tag=f"bank{PACK + t}") for t in range(PACK)]
        for h in range(2):
            for t in range(2):
                product(y[t][:, halves[h]], w1_q[0], slice(t * P, (t + 1) * P), xw[:, halves[h]], xs[:, halves[h]])
        for t in range(2):
            product(y[2 + t][:], w1_q[1], slice(t * P, (t + 1) * P), xw[:], xs[:])

        eo = [sbuf([P, S], F32, f"eo{t}") for t in range(PACK)]
        dif = sbuf([P, PACK * S], F32, "dif")
        for t in range(PACK):
            for on_vector, lo, hi in ORG_PLAN[t]:
                window = ye_sb[t][:].indirect(org_t[:, lo // STRIPE : hi // STRIPE])
                if on_vector:
                    nc.vector.tensor_copy(eo[t][:, lo:hi], window)
                else:
                    nc.scalar.activation(eo[t][:, lo:hi], window, ACT.Copy)
            nc.vector.scalar_tensor_tensor(dif[:, t * S : (t + 1) * S], y[t][:], unit_abs[:, t : t + 1], eo[t][:], ALU.mult, ALU.subtract)

        w3_b = sbuf([P, N, PACK], BF16, "w3_b", "eo0")
        nc.gpsimd.tensor_tensor(w3_b[:], w3_raw[:].rearrange("p j m -> p m j"),
                                unit_sign[:].unsqueeze(1).to_broadcast([P, N, PACK]), ALU.mult)

        scaled = sbuf([P, S], F32, "scaled", "eo2")
        nc.gpsimd.tensor_scalar(scaled[:], dif[:, 0:S], -0.8, 0.0, ALU.mult, ALU.add)

        ds = [sbuf([P, PACK * HALF], F32, f"ds{h}") for h in range(2)]
        for on_vector, t, lo, hi in SIB_PLAN:
            places = sib_t[:, lo // STRIPE : hi // STRIPE]
            at = t * HALF + lo % HALF
            dst = ds[lo // HALF][:, at : at + hi - lo]
            if on_vector:
                nc.vector.tensor_copy(dst, scaled[:].indirect(places))
            else:
                nc.scalar.activation(dst, dif[:, t * S : (t + 1) * S].indirect(places), ACT.Copy, scale=-0.8)
        def larger(c):
            lo, hi = CHUNKS[c]
            hid = sbuf([P, hi - lo, PACK], BF16, f"hid{c}")
            at = lo % HALF // 2
            nc.vector.tensor_tensor(hid[:].rearrange("p (c i) t -> p c t i", i=2),
                                    dif[:].rearrange("p (t c i) -> p c t i", t=PACK, i=2)[:, lo // 2 : hi // 2],
                                    ds[lo // HALF][:].rearrange("p (t c i) -> p c t i", t=PACK, i=2)[:, at : at + (hi - lo) // 2], ALU.max)
            return hid

        def finish(c, hid, w3_q):
            lo, hi = CHUNKS[c]
            hid_q = quantize(hid[:].rearrange("p c t -> p (c t)"), hi - lo, f"hid_q{c}")
            bank = psum.tile([P, hi - lo], F32, name=f"o{c}", tag=f"bank{c}")
            product(bank[:], w3_q, slice(0, N), hid_q[0][:], hid_q[1][:])
            res = sbuf([P, hi - lo], F32, f"res{c}")
            nc.scalar.copy(res[:], bank[:])
            nc.sync.dma_start(out[:, lo:hi], res[:])

        hid0 = larger(0)
        w3_q = quantize(w3_b[:].rearrange("p m j -> p (m j)"), N, "w3_q", "ds0")
        finish(0, hid0, w3_q)
        rest = [larger(c) for c in (1, 2)]
        for c in (1, 2):
            finish(c, rest[c - 1], w3_q)
